import numpy as np
import ml_dtypes

BF16 = ml_dtypes.bfloat16


def bf(x):
    return np.asarray(x, np.float32).astype(BF16)


def f32(x):
    return np.asarray(x, np.float32)


def f64(x):
    return np.asarray(x).astype(np.float64)


def striped(idx):
    return np.tile(idx.reshape(-1, 16).T, (8, 1))


S, K, M, N, E, Q, O = 256, 256, 256, 256, 2, 128, 512


def setup_inputs():
    return {"base": bf(np.random.standard_normal((M, S))), "x": bf(np.random.standard_normal((K, N))), "w": bf(1.2 * np.random.standard_normal((E, K, M)) / np.sqrt(K)), "w2": bf(np.random.standard_normal((M, O)) / np.sqrt(2 * M)), "b": f32(0.5 * np.random.standard_normal((O, 1))), "offs": striped(np.random.permutation(S))}


def reference(base, x, w, w2, b, offs):
    idx = offs[:16].T.reshape(-1)
    z = f64(base).copy()
    for e in range(E):
        z[:, idx[e * Q : (e + 1) * Q]] += f64(w)[e].T @ f64(x)[:, e * Q : (e + 1) * Q]
    y = f64(w2).T @ z
    return np.maximum(y + f64(b), 0.0)

@@ -1,0 +1,76 @@
+import concourse.mybir as mybir
+from concourse.masks import make_identity
+
+BF16, F32, U16 = mybir.dt.bfloat16, mybir.dt.float32, mybir.dt.uint16
+RELU = mybir.ActivationFunctionType.Relu
+ADD, MAX = mybir.AluOpType.add, mybir.AluOpType.max
+
+P = 128
+S, K, M, E, O = 256, 256, 256, 2, 512
+N = S
+Q = N // E
+KB, MB, OB = K // P, M // P, O // P
+COLS = Q // 16
+
+FLOPS = 2 * N * K * M + 2 * S * M * O
+
+
+def tile_rows_thenproj_relu_kernel(tc, base, x, w, w2, b, offs, out):
+    nc = tc.nc
+    with (
+        tc.tile_pool(name="sbuf", bufs=1) as sbuf,
+        tc.psum_pool(name="psum", bufs=1) as psum,
+    ):
+        base_t = sbuf.tile([P, MB, S], BF16)
+        offsets = sbuf.tile([P, N // 16], U16)
+        x_t = sbuf.tile([P, KB, N], BF16)
+        w_t = sbuf.tile([P, E, KB, M], BF16)
+        w2_t = sbuf.tile([P, MB, O], BF16)
+        bias = sbuf.tile([P, OB], F32)
+        ident = sbuf.tile([P, P], BF16)
+
+        nc.sync.dma_start(base_t[:], base.rearrange("(mb p) s -> p mb s", p=P))
+        nc.sync.dma_start(offsets[:], offs)
+        nc.sync.dma_start(x_t[:], x.rearrange("(p kb) n -> p kb n", kb=KB))
+        nc.sync.dma_start(w_t[:], w.rearrange("e (p kb) m -> p e kb m", kb=KB))
+        nc.sync.dma_start(w2_t[:], w2.rearrange("(mb p) o -> p mb o", p=P))
+        nc.sync.dma_start(bias[:], b.rearrange("(ob p) one -> p (ob one)", p=P))
+        make_identity(nc, ident[:])
+
+        windows = [psum.tile([P, S], F32, name=f"window{mb}") for mb in range(MB)]
+        for mb in range(MB):
+            nc.tensor.matmul(windows[mb][:], ident[:], base_t[:, mb, :], start=True, stop=False)
+
+        for e in range(E):
+            for mb in range(MB):
+                for kb in range(KB):
+                    nc.tensor.matmul(
+                        windows[mb][:].indirect(offsets[:, e * COLS : (e + 1) * COLS]),
+                        w_t[:, e, kb, mb * P : (mb + 1) * P],
+                        x_t[:, kb, e * Q : (e + 1) * Q],
+                        start=False,
+                        stop=(e == E - 1 and kb == KB - 1),
+                    )
+
+        z_t = [sbuf.tile([P, S], BF16, name=f"z{mb}") for mb in range(MB)]
+        nc.scalar.copy(z_t[0][:], windows[0][:])
+        nc.vector.tensor_copy(z_t[1][:], windows[1][:])
+
+        y_t = [psum.tile([P, S], F32, name=f"y{ob}") for ob in range(OB)]
+        for mb in range(MB):
+            for ob in range(OB):
+                nc.tensor.matmul(
+                    y_t[ob][:],
+                    w2_t[:, mb, ob * P : (ob + 1) * P],
+                    z_t[mb][:],
+                    start=(mb == 0),
+                    stop=(mb == MB - 1),
+                )
+
+        for ob in range(OB):
+            relu_t = sbuf.tile([P, S], F32, name=f"relu{ob}")
+            if ob % 2 == 0:
+                nc.scalar.activation(relu_t[:], y_t[ob][:], RELU, bias=bias[:, ob : ob + 1])
+            else:
+                nc.vector.tensor_scalar(relu_t[:], y_t[ob][:], bias[:, ob : ob + 1], 0.0, ADD, MAX)
+            nc.sync.dma_start(out[ob * P : (ob + 1) * P, :], relu_t[:])

@@ -11,6 +11,8 @@ N = S
 Q = N // E
 KB, MB, OB = K // P, M // P, O // P
 COLS = Q // 16
+BANK = 512
+WARM_UPS = 4
 
 FLOPS = 2 * N * K * M + 2 * S * M * O
 
@@ -36,6 +38,16 @@ def tile_rows_thenproj_relu_kernel(tc, base, x, w, w2, b, offs, out):
         nc.sync.dma_start(w2_t[:], w2.rearrange("(mb p) o -> p mb o", p=P))
         nc.sync.dma_start(bias[:], b.rearrange("(ob p) one -> p (ob one)", p=P))
         make_identity(nc, ident[:])
+
+        zeros = sbuf.tile([P, BANK], BF16)
+        zero_column = sbuf.tile([P, 1], F32)
+        unread_column = sbuf.tile([P, 1], F32)
+        unread_bank = psum.tile([P, BANK], F32)
+        nc.vector.memset(zeros[:], 0.0)
+        nc.vector.memset(zero_column[:], 0.0)
+        nc.scalar.activation(unread_column[:], zero_column[:], RELU, bias=zero_column[:])
+        for warm_up in range(WARM_UPS):
+            nc.tensor.matmul(unread_bank[:], zeros[:, :P], zeros[:], start=True, stop=True)
 
         windows = [psum.tile([P, S], F32, name=f"window{mb}") for mb in range(MB)]
         for mb in range(MB):

@@ -26,7 +26,7 @@ def tile_rows_thenproj_relu_kernel(tc, base, x, w, w2, b, offs, out):
         base_t = sbuf.tile([P, MB, S], BF16)
         offsets = sbuf.tile([P, N // 16], U16)
         x_t = sbuf.tile([P, KB, N], BF16)
-        w_t = sbuf.tile([P, E, KB, M], BF16)
+        w_t = [sbuf.tile([P, KB, M], BF16, name=f"w{e}") for e in range(E)]
         w2_t = sbuf.tile([P, MB, O], BF16)
         bias = sbuf.tile([P, OB], F32)
         ident = sbuf.tile([P, P], BF16)
@@ -34,7 +34,8 @@ def tile_rows_thenproj_relu_kernel(tc, base, x, w, w2, b, offs, out):
         nc.sync.dma_start(base_t[:], base.rearrange("(mb p) s -> p mb s", p=P))
         nc.sync.dma_start(offsets[:], offs)
         nc.sync.dma_start(x_t[:], x.rearrange("(p kb) n -> p kb n", kb=KB))
-        nc.sync.dma_start(w_t[:], w.rearrange("e (p kb) m -> p e kb m", kb=KB))
+        for e in range(E):
+            nc.sync.dma_start(w_t[e][:], w[e].rearrange("(p kb) m -> p kb m", kb=KB))
         nc.sync.dma_start(w2_t[:], w2.rearrange("(mb p) o -> p mb o", p=P))
         nc.sync.dma_start(bias[:], b.rearrange("(ob p) one -> p (ob one)", p=P))
         make_identity(nc, ident[:])
@@ -53,12 +54,12 @@ def tile_rows_thenproj_relu_kernel(tc, base, x, w, w2, b, offs, out):
         for mb in range(MB):
             nc.tensor.matmul(windows[mb][:], ident[:], base_t[:, mb, :], start=True, stop=False)
 
-        for e in range(E):
-            for mb in range(MB):
+        for mb in range(MB):
+            for e in range(E):
                 for kb in range(KB):
                     nc.tensor.matmul(
                         windows[mb][:].indirect(offsets[:, e * COLS : (e + 1) * COLS]),
-                        w_t[:, e, kb, mb * P : (mb + 1) * P],
+                        w_t[e][:, kb, mb * P : (mb + 1) * P],
                         x_t[:, kb, e * Q : (e + 1) * Q],
                         start=False,
                         stop=(e == E - 1 and kb == KB - 1),
@@ -82,7 +83,7 @@ def tile_rows_thenproj_relu_kernel(tc, base, x, w, w2, b, offs, out):
         for ob in range(OB):
             relu_t = sbuf.tile([P, S], F32, name=f"relu{ob}")
             if ob % 2 == 0:
-                nc.scalar.activation(relu_t[:], y_t[ob][:], RELU, bias=bias[:, ob : ob + 1])
-            else:
                 nc.vector.tensor_scalar(relu_t[:], y_t[ob][:], bias[:, ob : ob + 1], 0.0, ADD, MAX)
+            else:
+                nc.scalar.activation(relu_t[:], y_t[ob][:], RELU, bias=bias[:, ob : ob + 1])
             nc.sync.dma_start(out[ob * P : (ob + 1) * P, :], relu_t[:])

@@ -31,13 +31,13 @@ def tile_rows_thenproj_relu_kernel(tc, base, x, w, w2, b, offs, out):
         bias = sbuf.tile([P, OB], F32)
         ident = sbuf.tile([P, P], BF16)
 
-        nc.sync.dma_start(base_t[:], base.rearrange("(mb p) s -> p mb s", p=P))
+        nc.sync.dma_start(base_t[:], base.rearrange("(p mb) s -> p mb s", mb=MB))
         nc.sync.dma_start(offsets[:], offs)
         nc.sync.dma_start(x_t[:], x.rearrange("(p kb) n -> p kb n", kb=KB))
         for e in range(E):
             nc.sync.dma_start(w_t[e][:], w[e].rearrange("(p kb) m -> p kb m", kb=KB))
-        nc.sync.dma_start(w2_t[:], w2.rearrange("(mb p) o -> p mb o", p=P))
-        nc.sync.dma_start(bias[:], b.rearrange("(ob p) one -> p (ob one)", p=P))
+        nc.sync.dma_start(w2_t[:], w2.rearrange("(p mb) o -> p mb o", mb=MB))
+        nc.sync.dma_start(bias[:], b.rearrange("(p ob) one -> p (ob one)", ob=OB))
         make_identity(nc, ident[:])
 
         zeros = sbuf.tile([P, BANK], BF16)
@@ -59,7 +59,7 @@ def tile_rows_thenproj_relu_kernel(tc, base, x, w, w2, b, offs, out):
                 for kb in range(KB):
                     nc.tensor.matmul(
                         windows[mb][:].indirect(offsets[:, e * COLS : (e + 1) * COLS]),
-                        w_t[e][:, kb, mb * P : (mb + 1) * P],
+                        w_t[e][:, kb, mb::MB],
                         x_t[:, kb, e * Q : (e + 1) * Q],
                         start=False,
                         stop=(e == E - 1 and kb == KB - 1),
@@ -74,16 +74,17 @@ def tile_rows_thenproj_relu_kernel(tc, base, x, w, w2, b, offs, out):
             for ob in range(OB):
                 nc.tensor.matmul(
                     y_t[ob][:],
-                    w2_t[:, mb, ob * P : (ob + 1) * P],
+                    w2_t[:, mb, ob::OB],
                     z_t[mb][:],
                     start=(mb == 0),
                     stop=(mb == MB - 1),
                 )
 
+        out_blocks = out.rearrange("(p ob) i -> ob p i", ob=OB)
         for ob in range(OB):
             relu_t = sbuf.tile([P, S], F32, name=f"relu{ob}")
             if ob % 2 == 0:
                 nc.vector.tensor_scalar(relu_t[:], y_t[ob][:], bias[:, ob : ob + 1], 0.0, ADD, MAX)
             else:
                 nc.scalar.activation(relu_t[:], y_t[ob][:], RELU, bias=bias[:, ob : ob + 1])
-            nc.sync.dma_start(out[ob * P : (ob + 1) * P, :], relu_t[:])
+            nc.sync.dma_start(out_blocks[ob], relu_t[:])

import concourse.mybir as mybir
from concourse.masks import make_identity

BF16, F32, U16 = mybir.dt.bfloat16, mybir.dt.float32, mybir.dt.uint16
RELU = mybir.ActivationFunctionType.Relu
ADD, MAX = mybir.AluOpType.add, mybir.AluOpType.max

P = 128
S, K, M, E, O = 256, 256, 256, 2, 512
N = S
Q = N // E
KB, MB, OB = K // P, M // P, O // P
COLS = Q // 16
BANK = 512
WARM_UPS = 4

FLOPS = 2 * N * K * M + 2 * S * M * O


def tile_rows_thenproj_relu_kernel(tc, base, x, w, w2, b, offs, out):
    nc = tc.nc
    with (
        tc.tile_pool(name="sbuf", bufs=1) as sbuf,
        tc.psum_pool(name="psum", bufs=1) as psum,
    ):
        base_t = sbuf.tile([P, MB, S], BF16)
        offsets = sbuf.tile([P, N // 16], U16)
        x_t = sbuf.tile([P, KB, N], BF16)
        w_t = [sbuf.tile([P, KB, M], BF16, name=f"w{e}") for e in range(E)]
        w2_t = sbuf.tile([P, MB, O], BF16)
        bias = sbuf.tile([P, OB], F32)
        ident = sbuf.tile([P, P], BF16)

        nc.sync.dma_start(base_t[:], base.rearrange("(p mb) s -> p mb s", mb=MB))
        nc.sync.dma_start(offsets[:], offs)
        nc.sync.dma_start(x_t[:], x.rearrange("(p kb) n -> p kb n", kb=KB))
        for e in range(E):
            nc.sync.dma_start(w_t[e][:], w[e].rearrange("(p kb) m -> p kb m", kb=KB))
        nc.sync.dma_start(w2_t[:], w2.rearrange("(p mb) o -> p mb o", mb=MB))
        nc.sync.dma_start(bias[:], b.rearrange("(p ob) one -> p (ob one)", ob=OB))
        make_identity(nc, ident[:])

        zeros = sbuf.tile([P, BANK], BF16)
        zero_column = sbuf.tile([P, 1], F32)
        unread_column = sbuf.tile([P, 1], F32)
        unread_bank = psum.tile([P, BANK], F32)
        nc.vector.memset(zeros[:], 0.0)
        nc.vector.memset(zero_column[:], 0.0)
        nc.scalar.activation(unread_column[:], zero_column[:], RELU, bias=zero_column[:])
        for warm_up in range(WARM_UPS):
            nc.tensor.matmul(unread_bank[:], zeros[:, :P], zeros[:], start=True, stop=True)

        windows = [psum.tile([P, S], F32, name=f"window{mb}") for mb in range(MB)]
        for mb in range(MB):
            nc.tensor.matmul(windows[mb][:], ident[:], base_t[:, mb, :], start=True, stop=False)

        for mb in range(MB):
            for e in range(E):
                for kb in range(KB):
                    nc.tensor.matmul(
                        windows[mb][:].indirect(offsets[:, e * COLS : (e + 1) * COLS]),
                        w_t[e][:, kb, mb::MB],
                        x_t[:, kb, e * Q : (e + 1) * Q],
                        start=False,
                        stop=(e == E - 1 and kb == KB - 1),
                    )

        z_t = [sbuf.tile([P, S], BF16, name=f"z{mb}") for mb in range(MB)]
        nc.scalar.copy(z_t[0][:], windows[0][:])
        nc.vector.tensor_copy(z_t[1][:], windows[1][:])

        y_t = [psum.tile([P, S], F32, name=f"y{ob}") for ob in range(OB)]
        for mb in range(MB):
            for ob in range(OB):
                nc.tensor.matmul(
                    y_t[ob][:],
                    w2_t[:, mb, ob::OB],
                    z_t[mb][:],
                    start=(mb == 0),
                    stop=(mb == MB - 1),
                )

        out_blocks = out.rearrange("(p ob) i -> ob p i", ob=OB)
        for ob in range(OB):
            relu_t = sbuf.tile([P, S], F32, name=f"relu{ob}")
            if ob % 2 == 0:
                nc.vector.tensor_scalar(relu_t[:], y_t[ob][:], bias[:, ob : ob + 1], 0.0, ADD, MAX)
            else:
                nc.scalar.activation(relu_t[:], y_t[ob][:], RELU, bias=bias[:, ob : ob + 1])
            nc.sync.dma_start(out_blocks[ob], relu_t[:])
